import numpy as np, ml_dtypes
CORES = [50,106,114,52,108,116]
N = 6
V, K = 1024, 4
T = V * K; R = V
def entries(a): return a.T.reshape(-1)
def pack(v, P): return np.ascontiguousarray(np.asarray(v, np.int32).reshape(-1, P).T)
def lists(rng, how):
    I = rng.integers(0, N * R, (N, T))
    if how == "alike": I[:] = rng.integers(0, N * R, (N, 1))
    if how == "self": I = (R * np.arange(N).reshape(N, 1) + np.arange(T).reshape(1, T) // K)
    if how == "hotrank": I = R * int(rng.integers(N)) + rng.integers(0, R, (N, T))
    if how == "own": I = R * np.arange(N).reshape(N, 1) + rng.integers(0, R, (N, T))
    if how == "edge": I = R * rng.integers(0, N, (N, T)) + np.where(rng.random((N, T)) < 0.5, 0, R - 1)
    return {"nb": np.stack([pack(I[r], 16) for r in range(N)])}
def setup_inputs(rng):
    w = (rng.standard_normal((128, 128), dtype=np.float32) / 16).astype(ml_dtypes.bfloat16)
    return dict({"x": rng.standard_normal((N, 128, V), dtype=np.float32).astype(ml_dtypes.bfloat16), "w": np.broadcast_to(w, (N, 128, 128)).copy()}, **lists(rng, "uniform"))
def setup_inputs_alike(rng):
    d = setup_inputs(rng); d.update(lists(rng, "alike"))
    for k in ("x",): d[k] = (d[k].astype(np.float32) * 1024.0).astype(d[k].dtype)
    return d
def setup_inputs_edge(rng):
    d = setup_inputs(rng); d.update(lists(rng, "edge"))
    for k in ("x",): d[k] = (d[k].astype(np.float32) * (1 / 1024.0)).astype(d[k].dtype)
    return d
def setup_inputs_hotrank(rng):
    d = setup_inputs(rng); d.update(lists(rng, "hotrank"))
    return d
def setup_inputs_own(rng):
    d = setup_inputs(rng); d.update(lists(rng, "own"))
    return d
def setup_inputs_self(rng):
    d = setup_inputs(rng); d.update(lists(rng, "self"))
    return d
def check_inputs(x):
    bad = []
    if x["nb"].min() < 0 or x["nb"].max() >= N * V: bad.append("nb out of range")
    if not all(np.array_equal(a, x["w"][0]) for a in x["w"]): bad.append("w isn't alike on all ranks")
    return bad
def reference(x, w, nb):
    X, W = x.astype(np.float64), w.astype(np.float64)
    A = np.concatenate(list(X), axis=1)
    return {"y": np.stack([np.maximum(W[r].T @ (X[r] + A[:, entries(nb[r])].reshape(128, V, K).sum(axis=2)), 0.0) for r in range(N)]).astype(ml_dtypes.bfloat16)}

@@ -1,0 +1,245 @@
+from concourse.bass import DstId, RemoteDMATransfer
+from concourse.mybir import AluOpType, ActivationFunctionType
+
+N, V = 6, 1024
+NCH = 2
+W = V // NCH
+DETOUR = ()
+TWICE_PASSED = False
+TWICE_DIRECT = False
+BLOCKS = [128, 256, 256, 256, 128]
+STORES = [[0], [1], [2], [3], [4]]
+
+SCRATCH = {
+    "win": ("sbuf", [128, N * V], "bfloat16"),
+    "wsb": ("sbuf", [128, 128], "bfloat16"),
+    "nbi": ("sbuf", [128, 256], "int32"),
+    "nbf": ("sbuf", [128, 256], "float32"),
+    "iot": ("sbuf", [128, 128], "float32"),
+    "sel": ("sbuf", [128, 512], "float32"),
+    "off": ("sbuf", [128, 256], "uint16"),
+    "gat": ("sbuf", [128, 2 * V], "bfloat16"),
+    "hsum": ("sbuf", [128, 2 * V], "bfloat16"),
+    "ysb": ("sbuf", [128, V], "bfloat16"),
+    "pso": ("psum", [128, 512], "float32"),
+}
+for _i in range(len(BLOCKS)):
+    SCRATCH["ps%d" % _i] = ("psum", [128, 512], "float32")
+
+SEMAPHORES = (["ldx%d" % c for c in range(NCH)] + ["ldw", "ldnb", "sent", "vi", "vs", "po", "vo", "st"]
+              + ["a%d_%d" % (s, c) for s in range(N) for c in range(NCH)]
+              + ["%s%d" % (n, i) for n in ("gd", "hd", "pd", "rd") for i in range(len(BLOCKS))])
+
+
+def _bits(m):
+    return [i for i in range(32) if (m >> i) & 1]
+
+
+def _mask(engines):
+    m = 0
+    for e in engines:
+        m |= 1 << e
+    return m
+
+
+def _share(pool, m):
+    k = 1
+    while 2 * k * m <= len(pool):
+        k *= 2
+    return [pool[i * k:(i + 1) * k] for i in range(m)]
+
+
+def _paths(cores, topo):
+    everyone = range(topo.CHIPS * topo.CORES_PER_CHIP)
+    chips = sorted(set(topo.chip(c) for c in cores))
+    used = set(cores)
+    helper = {}
+    enters = {}
+    paths = {}
+
+    def port(path, X):
+        return (X, topo.die(path[-2]), topo.mates(topo.chip(path[-2]), X))
+
+    def passer(s, X, t, near):
+        if (s, X, near) not in helper:
+            free = [h for h in everyone if h not in used and topo.die(h) == topo.die(s)
+                    and topo.may_write(s, h) and topo.may_write(h, t)
+                    and (topo.chip(h) == topo.chip(s) if near else topo.mates(topo.chip(h), X))]
+            helper[(s, X, near)] = free[0] if free else None
+            used.add(helper[(s, X, near)])
+        return helper[(s, X, near)]
+
+    for c in range(NCH):
+        todo = []
+        for s in cores:
+            for X in chips:
+                if X == topo.chip(s):
+                    continue
+                there = [p for p in cores if topo.chip(p) == X]
+                t = ([p for p in there if topo.die(p) == topo.die(s)] + there)[0]
+                ways = [[s, t]] if topo.may_write(s, t) else [[s, passer(s, X, t, True), t]]
+                if not topo.same_plane(topo.chip(s), X) and (c in DETOUR or not topo.may_write(s, t)):
+                    ways.append([s, passer(s, X, t, False), t])
+                todo.append((len(ways), s, X, [w for w in ways if None not in w]))
+        for _n, s, X, ways in sorted(todo, key=lambda x: x[0]):
+            path = min(ways, key=lambda w: enters.get(port(w, X), 0))
+            paths[(s, X, c)] = path
+            enters[port(path, X)] = enters.get(port(path, X), 0) + 1
+    return paths
+
+
+def _when(call):
+    r, c0, c1, depth, deal = call
+    return (0, depth, c0, r) if depth < 1 else (1, c0 + depth, depth, r)
+
+
+def _plan(cores, topo):
+    kids = {}
+
+    def edge(a, b, r, c, depth):
+        kids.setdefault((a, r, c), (depth, []))[1].append(b)
+
+    for (s, X, c), path in sorted(_paths(cores, topo).items()):
+        r = cores.index(s)
+        rest = [p for p in cores if p != path[-1] and topo.chip(p) == X]
+        for d in range(len(path) - 1):
+            edge(path[d], path[d + 1], r, c, d)
+        twice = TWICE_PASSED if len(path) > 2 else TWICE_DIRECT
+        for p in rest:
+            if twice and topo.may_write(path[-2], p):
+                edge(path[-2], p, r, c, len(path) - 2)
+            else:
+                edge(path[-1], p, r, c, len(path) - 1)
+    sends, lands = {}, {}
+
+    def call(a, r, c0, c1, depth, deal):
+        sends.setdefault(a, []).append((r, c0, c1, depth, deal))
+        for d, eng in deal:
+            lands.setdefault(d, {})["a%d_%d" % (r, c0)] = len(eng)
+
+    def engines(a):
+        away = [c for c in cores if topo.chip(c) != topo.chip(a)][0]
+        home = [c for c in range(topo.CHIPS * topo.CORES_PER_CHIP) if c != a and topo.chip(c) == topo.chip(a)][0]
+        lo = _bits(topo.mask(a, away))
+        return lo, [e for e in _bits(topo.mask(a, home)) if e not in lo]
+
+    for (a, r, c), (depth, dsts) in kids.items():
+        lo, hi = engines(a)
+        home = [d for d in dsts if d in cores and topo.chip(d) == topo.chip(a)]
+        urgent = [d for d in dsts if d not in home]
+        if urgent:
+            call(a, r, c, c + 1, depth, list(zip(urgent, _share(lo, len(urgent)))))
+        if home:
+            call(a, r, c, c + 1, depth, list(zip(home, _share(hi, len(home)))))
+    for r, s in enumerate(cores):
+        home = [p for p in cores if p != s and topo.chip(p) == topo.chip(s)]
+        if home:
+            call(s, r, 0, NCH, 0.5, list(zip(home, _share(engines(s)[1], len(home)))))
+    for a in sends:
+        sends[a].sort(key=_when)
+    return sends, lands
+
+
+def _cols(r, c0, c1):
+    return slice(r * V + c0 * W, r * V + c1 * W)
+
+
+def _comms(g, core, T, topo, sends, lands, rank):
+    total = 0
+    for r, c0, c1, depth, deal in sends.get(core, []):
+        name = "a%d_%d" % (r, c0)
+        if r == rank:
+            for c in range(c0, c1):
+                g.wait_ge(T.sem["ldx%d" % c], 16)
+        else:
+            g.wait_ge(T.sem[name], lands[core][name])
+        piece = T.win[:, _cols(r, c0, c1)]
+        trs = []
+        for d, eng in deal:
+            rid, pid, _se = topo.addr(d)
+            trs.append(RemoteDMATransfer(dst_ids=[DstId(rid=rid, pnc=pid)], dma_engine_mask=_mask(eng),
+                                         remote_sem=T.sem[name], src=piece, dst=piece))
+            total += len(eng)
+        g.remote_dma_fused(trs, local_sem=T.sem.sent)
+    if total:
+        g.wait_ge(T.sem.sent, total)
+
+
+def rank_program(g, core, T, topo):
+    cores = list(T.cores)
+    rank = T.rank_of(core)
+    sends, lands = _plan(cores, topo)
+    if rank is None:
+        _comms(g, core, T, topo, sends, lands, None)
+        return
+    sem = T.sem
+    nblk = len(BLOCKS)
+    lo = [sum(BLOCKS[:i]) for i in range(nblk)]
+    ps = [T["ps%d" % i] for i in range(nblk)]
+
+    for c in range(NCH):
+        q = g.sync if c % 2 == 0 else g.scalar
+        q.dma_start(T.win[:, _cols(rank, c, c + 1)], T.x[:, c * W:(c + 1) * W]).then_inc(sem["ldx%d" % c], 16)
+    g.sync.dma_start(T.nbi[0:16, :], T.nb[:, :]).then_inc(sem.ldnb, 16)
+    g.scalar.dma_start(T.wsb[:, :], T.w[:, :]).then_inc(sem.ldw, 16)
+
+    g.iota(T.iot[0:16, :], [[0, 8], [-4, 8], [-1, 2]], 0, 1, allow_small_or_imprecise_dtypes=True).then_inc(sem.vi, 1)
+    _comms(g, core, T, topo, sends, lands, rank)
+
+    v = g.vector
+    v.wait_ge(sem.vi, 1)
+    for u in range(2):
+        for h in range(2):
+            i = 2 * u + h
+            v.tensor_scalar(T.sel[0:16, i * 128:(i + 1) * 128], T.iot[0:16, :], float(2 * u - 16 * h), None,
+                            AluOpType.is_equal).then_inc(sem.vs, 1)
+    v.wait_ge(sem.ldnb, 16)
+    for h in range(2):
+        v.tensor_copy(T.nbf[0:16, h * 128:(h + 1) * 128], T.nbi[0:16, h:256:2]).then_inc(sem.vs, 1)
+    pe = g.tensor
+    pe.wait_ge(sem.vs, 6)
+    for u in range(2):
+        for h in range(2):
+            i = 2 * u + h
+            pe.matmul(T.pso[:, u * 128:(u + 1) * 128], T.sel[0:16, i * 128:(i + 1) * 128],
+                      T.nbf[0:16, h * 128:(h + 1) * 128], h == 0, h == 1).then_inc(sem.po, 1)
+    v.wait_ge(sem.po, 4)
+    v.tensor_copy(T.off[:, :], T.pso[:, 0:256]).then_inc(sem.vo, 1)
+
+    pe.wait_ge(sem.ldw, 16)
+    for c in range(NCH):
+        pe.wait_ge(sem["ldx%d" % c], 16)
+    for i in range(nblk):
+        a = rank * V + lo[i]
+        pe.matmul(ps[i][:, 0:BLOCKS[i]], T.wsb[:, :], T.win[:, a:a + BLOCKS[i]], True, False).then_inc(sem["pd%d" % i], 1)
+
+    for q in (g.scalar, v):
+        q.wait_ge(sem.vo, 1)
+        for c in range(NCH):
+            q.wait_ge(sem["ldx%d" % c], 16)
+        for name in sorted(lands[core]):
+            q.wait_ge(sem[name], lands[core][name])
+    for i in range(nblk):
+        a, b = lo[i], lo[i] + BLOCKS[i]
+        first = T.win[:, :].indirect(T.off[:, a // 8:b // 8])
+        if i == 0:
+            v.tensor_copy(T.gat[:, 2 * a:2 * b], first).then_inc(sem["gd%d" % i], 1)
+        else:
+            g.scalar.activation(T.gat[:, 2 * a:2 * b], first, ActivationFunctionType.Copy).then_inc(sem["gd%d" % i], 1)
+        v.wait_ge(sem["gd%d" % i], 1)
+        v.tensor_tensor(T.hsum[:, 2 * a:2 * b], T.win[:, :].indirect(T.off[:, 128 + a // 8:128 + b // 8]),
+                        T.gat[:, 2 * a:2 * b], AluOpType.add).then_inc(sem["hd%d" % i], 1)
+        pe.wait_ge(sem["hd%d" % i], 1)
+        for k in range(2):
+            pe.matmul(ps[i][:, 0:BLOCKS[i]], T.wsb[:, :], T.hsum[:, 2 * a + k:2 * b:2], False, k == 1).then_inc(
+                sem["pd%d" % i], 1)
+    for i in range(nblk):
+        a, b = lo[i], lo[i] + BLOCKS[i]
+        g.scalar.wait_ge(sem["pd%d" % i], 3)
+        g.scalar.activation(T.ysb[:, a:b], ps[i][:, 0:BLOCKS[i]], ActivationFunctionType.Relu).then_inc(sem["rd%d" % i], 1)
+    for grp in STORES:
+        for i in grp:
+            g.sync.wait_ge(sem["rd%d" % i], 1)
+        a, b = lo[grp[0]], lo[grp[-1]] + BLOCKS[grp[-1]]
+        g.sync.dma_start(T.y[:, a:b], T.ysb[:, a:b]).then_inc(sem.st, 16)
+    g.sync.wait_ge(sem.st, 16 * len(STORES))

@@ -2,11 +2,11 @@ from concourse.bass import DstId, RemoteDMATransfer
 from concourse.mybir import AluOpType, ActivationFunctionType
 
 N, V = 6, 1024
-NCH = 2
-W = V // NCH
-DETOUR = ()
-TWICE_PASSED = False
-TWICE_DIRECT = False
+CH = [128, 512, 384]
+NCH = len(CH)
+AT = [sum(CH[:c]) for c in range(NCH + 1)]
+DETOUR = (0, 1)
+TWICE = (NCH - 1,)
 BLOCKS = [128, 256, 256, 256, 128]
 STORES = [[0], [1], [2], [3], [4]]
 
@@ -84,37 +84,30 @@ def _paths(cores, topo):
         for _n, s, X, ways in sorted(todo, key=lambda x: x[0]):
             path = min(ways, key=lambda w: enters.get(port(w, X), 0))
             paths[(s, X, c)] = path
-            enters[port(path, X)] = enters.get(port(path, X), 0) + 1
+            enters[port(path, X)] = enters.get(port(path, X), 0) + CH[c]
     return paths
-
-
-def _when(call):
-    r, c0, c1, depth, deal = call
-    return (0, depth, c0, r) if depth < 1 else (1, c0 + depth, depth, r)
 
 
 def _plan(cores, topo):
     kids = {}
 
-    def edge(a, b, r, c, depth):
-        kids.setdefault((a, r, c), (depth, []))[1].append(b)
+    def edge(a, b, r, c):
+        kids.setdefault((a, r, c), []).append(b)
 
     for (s, X, c), path in sorted(_paths(cores, topo).items()):
         r = cores.index(s)
-        rest = [p for p in cores if p != path[-1] and topo.chip(p) == X]
         for d in range(len(path) - 1):
-            edge(path[d], path[d + 1], r, c, d)
-        twice = TWICE_PASSED if len(path) > 2 else TWICE_DIRECT
-        for p in rest:
-            if twice and topo.may_write(path[-2], p):
-                edge(path[-2], p, r, c, len(path) - 2)
+            edge(path[d], path[d + 1], r, c)
+        for p in [p for p in cores if p != path[-1] and topo.chip(p) == X]:
+            if c in TWICE and len(path) > 2 and topo.may_write(path[-2], p):
+                edge(path[-2], p, r, c)
             else:
-                edge(path[-1], p, r, c, len(path) - 1)
+                edge(path[-1], p, r, c)
     sends, lands = {}, {}
 
-    def call(a, r, c0, c1, depth, deal):
-        sends.setdefault(a, []).append((r, c0, c1, depth, deal))
-        for d, eng in deal:
+    def call(a, key, trs):
+        sends.setdefault(a, []).append((key, trs))
+        for r, c0, c1, d, eng in trs:
             lands.setdefault(d, {})["a%d_%d" % (r, c0)] = len(eng)
 
     def engines(a):
@@ -123,42 +116,54 @@ def _plan(cores, topo):
         lo = _bits(topo.mask(a, away))
         return lo, [e for e in _bits(topo.mask(a, home)) if e not in lo]
 
-    for (a, r, c), (depth, dsts) in kids.items():
+    passed = {}
+    for (a, r, c), dsts in sorted(kids.items()):
         lo, hi = engines(a)
         home = [d for d in dsts if d in cores and topo.chip(d) == topo.chip(a)]
         urgent = [d for d in dsts if d not in home]
         if urgent:
-            call(a, r, c, c + 1, depth, list(zip(urgent, _share(lo, len(urgent)))))
-        if home:
-            call(a, r, c, c + 1, depth, list(zip(home, _share(hi, len(home)))))
+            call(a, (0, c, r), [(r, c, c + 1, d, e) for d, e in zip(urgent, _share(lo, len(urgent)))])
+        for d in home:
+            passed.setdefault(a, {}).setdefault(c, []).append((r, d))
     for r, s in enumerate(cores):
         home = [p for p in cores if p != s and topo.chip(p) == topo.chip(s)]
         if home:
-            call(s, r, 0, NCH, 0.5, list(zip(home, _share(engines(s)[1], len(home)))))
+            call(s, (0, NCH, r), [(r, 0, NCH, d, e) for d, e in zip(home, _share(engines(s)[1], len(home)))])
+    for a, by in sorted(passed.items()):
+        lo, hi = engines(a)
+        early = [x for x in by.get(0, []) if all(x in by.get(c, []) for c in range(NCH - 1))]
+        if early:
+            call(a, (1, 0), [(r, 0, NCH - 1, d, e) for (r, d), e in zip(early, _share(lo + hi, len(early)))])
+        for c in range(NCH):
+            rest = [x for x in by.get(c, []) if c == NCH - 1 or x not in early]
+            if rest:
+                call(a, (1, 1 + c), [(r, c, c + 1, d, e) for (r, d), e in zip(rest, _share(lo + hi, len(rest)))])
     for a in sends:
-        sends[a].sort(key=_when)
+        sends[a].sort(key=lambda x: x[0])
     return sends, lands
 
 
 def _cols(r, c0, c1):
-    return slice(r * V + c0 * W, r * V + c1 * W)
+    return slice(r * V + AT[c0], r * V + AT[c1])
 
 
 def _comms(g, core, T, topo, sends, lands, rank):
     total = 0
-    for r, c0, c1, depth, deal in sends.get(core, []):
-        name = "a%d_%d" % (r, c0)
-        if r == rank:
-            for c in range(c0, c1):
-                g.wait_ge(T.sem["ldx%d" % c], 16)
-        else:
-            g.wait_ge(T.sem[name], lands[core][name])
-        piece = T.win[:, _cols(r, c0, c1)]
+    for _key, deal in sends.get(core, []):
+        waited = set()
         trs = []
-        for d, eng in deal:
+        for r, c0, c1, d, eng in deal:
+            for c in range(c0, c1):
+                if (r, c) not in waited:
+                    waited.add((r, c))
+                    if r == rank:
+                        g.wait_ge(T.sem["ldx%d" % c], 16)
+                    else:
+                        g.wait_ge(T.sem["a%d_%d" % (r, c)], lands[core]["a%d_%d" % (r, c)])
+            piece = T.win[:, _cols(r, c0, c1)]
             rid, pid, _se = topo.addr(d)
             trs.append(RemoteDMATransfer(dst_ids=[DstId(rid=rid, pnc=pid)], dma_engine_mask=_mask(eng),
-                                         remote_sem=T.sem[name], src=piece, dst=piece))
+                                         remote_sem=T.sem["a%d_%d" % (r, c0)], src=piece, dst=piece))
             total += len(eng)
         g.remote_dma_fused(trs, local_sem=T.sem.sent)
     if total:
@@ -179,7 +184,7 @@ def rank_program(g, core, T, topo):
 
     for c in range(NCH):
         q = g.sync if c % 2 == 0 else g.scalar
-        q.dma_start(T.win[:, _cols(rank, c, c + 1)], T.x[:, c * W:(c + 1) * W]).then_inc(sem["ldx%d" % c], 16)
+        q.dma_start(T.win[:, _cols(rank, c, c + 1)], T.x[:, AT[c]:AT[c + 1]]).then_inc(sem["ldx%d" % c], 16)
     g.sync.dma_start(T.nbi[0:16, :], T.nb[:, :]).then_inc(sem.ldnb, 16)
     g.scalar.dma_start(T.wsb[:, :], T.w[:, :]).then_inc(sem.ldw, 16)
 

from concourse.bass import DstId, RemoteDMATransfer
from concourse.mybir import AluOpType, ActivationFunctionType

N, V = 6, 1024
CH = [128, 512, 384]
NCH = len(CH)
AT = [sum(CH[:c]) for c in range(NCH + 1)]
DETOUR = (0, 1)
TWICE = (NCH - 1,)
BLOCKS = [128, 256, 256, 256, 128]
STORES = [[0], [1], [2], [3], [4]]

SCRATCH = {
    "win": ("sbuf", [128, N * V], "bfloat16"),
    "wsb": ("sbuf", [128, 128], "bfloat16"),
    "nbi": ("sbuf", [128, 256], "int32"),
    "nbf": ("sbuf", [128, 256], "float32"),
    "iot": ("sbuf", [128, 128], "float32"),
    "sel": ("sbuf", [128, 512], "float32"),
    "off": ("sbuf", [128, 256], "uint16"),
    "gat": ("sbuf", [128, 2 * V], "bfloat16"),
    "hsum": ("sbuf", [128, 2 * V], "bfloat16"),
    "ysb": ("sbuf", [128, V], "bfloat16"),
    "pso": ("psum", [128, 512], "float32"),
}
for _i in range(len(BLOCKS)):
    SCRATCH["ps%d" % _i] = ("psum", [128, 512], "float32")

SEMAPHORES = (["ldx%d" % c for c in range(NCH)] + ["ldw", "ldnb", "sent", "vi", "vs", "po", "vo", "st"]
              + ["a%d_%d" % (s, c) for s in range(N) for c in range(NCH)]
              + ["%s%d" % (n, i) for n in ("gd", "hd", "pd", "rd") for i in range(len(BLOCKS))])


def _bits(m):
    return [i for i in range(32) if (m >> i) & 1]


def _mask(engines):
    m = 0
    for e in engines:
        m |= 1 << e
    return m


def _share(pool, m):
    k = 1
    while 2 * k * m <= len(pool):
        k *= 2
    return [pool[i * k:(i + 1) * k] for i in range(m)]


def _paths(cores, topo):
    everyone = range(topo.CHIPS * topo.CORES_PER_CHIP)
    chips = sorted(set(topo.chip(c) for c in cores))
    used = set(cores)
    helper = {}
    enters = {}
    paths = {}

    def port(path, X):
        return (X, topo.die(path[-2]), topo.mates(topo.chip(path[-2]), X))

    def passer(s, X, t, near):
        if (s, X, near) not in helper:
            free = [h for h in everyone if h not in used and topo.die(h) == topo.die(s)
                    and topo.may_write(s, h) and topo.may_write(h, t)
                    and (topo.chip(h) == topo.chip(s) if near else topo.mates(topo.chip(h), X))]
            helper[(s, X, near)] = free[0] if free else None
            used.add(helper[(s, X, near)])
        return helper[(s, X, near)]

    for c in range(NCH):
        todo = []
        for s in cores:
            for X in chips:
                if X == topo.chip(s):
                    continue
                there = [p for p in cores if topo.chip(p) == X]
                t = ([p for p in there if topo.die(p) == topo.die(s)] + there)[0]
                ways = [[s, t]] if topo.may_write(s, t) else [[s, passer(s, X, t, True), t]]
                if not topo.same_plane(topo.chip(s), X) and (c in DETOUR or not topo.may_write(s, t)):
                    ways.append([s, passer(s, X, t, False), t])
                todo.append((len(ways), s, X, [w for w in ways if None not in w]))
        for _n, s, X, ways in sorted(todo, key=lambda x: x[0]):
            path = min(ways, key=lambda w: enters.get(port(w, X), 0))
            paths[(s, X, c)] = path
            enters[port(path, X)] = enters.get(port(path, X), 0) + CH[c]
    return paths


def _plan(cores, topo):
    kids = {}

    def edge(a, b, r, c):
        kids.setdefault((a, r, c), []).append(b)

    for (s, X, c), path in sorted(_paths(cores, topo).items()):
        r = cores.index(s)
        for d in range(len(path) - 1):
            edge(path[d], path[d + 1], r, c)
        for p in [p for p in cores if p != path[-1] and topo.chip(p) == X]:
            if c in TWICE and len(path) > 2 and topo.may_write(path[-2], p):
                edge(path[-2], p, r, c)
            else:
                edge(path[-1], p, r, c)
    sends, lands = {}, {}

    def call(a, key, trs):
        sends.setdefault(a, []).append((key, trs))
        for r, c0, c1, d, eng in trs:
            lands.setdefault(d, {})["a%d_%d" % (r, c0)] = len(eng)

    def engines(a):
        away = [c for c in cores if topo.chip(c) != topo.chip(a)][0]
        home = [c for c in range(topo.CHIPS * topo.CORES_PER_CHIP) if c != a and topo.chip(c) == topo.chip(a)][0]
        lo = _bits(topo.mask(a, away))
        return lo, [e for e in _bits(topo.mask(a, home)) if e not in lo]

    passed = {}
    for (a, r, c), dsts in sorted(kids.items()):
        lo, hi = engines(a)
        home = [d for d in dsts if d in cores and topo.chip(d) == topo.chip(a)]
        urgent = [d for d in dsts if d not in home]
        if urgent:
            call(a, (0, c, r), [(r, c, c + 1, d, e) for d, e in zip(urgent, _share(lo, len(urgent)))])
        for d in home:
            passed.setdefault(a, {}).setdefault(c, []).append((r, d))
    for r, s in enumerate(cores):
        home = [p for p in cores if p != s and topo.chip(p) == topo.chip(s)]
        if home:
            call(s, (0, NCH, r), [(r, 0, NCH, d, e) for d, e in zip(home, _share(engines(s)[1], len(home)))])
    for a, by in sorted(passed.items()):
        lo, hi = engines(a)
        early = [x for x in by.get(0, []) if all(x in by.get(c, []) for c in range(NCH - 1))]
        if early:
            call(a, (1, 0), [(r, 0, NCH - 1, d, e) for (r, d), e in zip(early, _share(lo + hi, len(early)))])
        for c in range(NCH):
            rest = [x for x in by.get(c, []) if c == NCH - 1 or x not in early]
            if rest:
                call(a, (1, 1 + c), [(r, c, c + 1, d, e) for (r, d), e in zip(rest, _share(lo + hi, len(rest)))])
    for a in sends:
        sends[a].sort(key=lambda x: x[0])
    return sends, lands


def _cols(r, c0, c1):
    return slice(r * V + AT[c0], r * V + AT[c1])


def _comms(g, core, T, topo, sends, lands, rank):
    total = 0
    for _key, deal in sends.get(core, []):
        waited = set()
        trs = []
        for r, c0, c1, d, eng in deal:
            for c in range(c0, c1):
                if (r, c) not in waited:
                    waited.add((r, c))
                    if r == rank:
                        g.wait_ge(T.sem["ldx%d" % c], 16)
                    else:
                        g.wait_ge(T.sem["a%d_%d" % (r, c)], lands[core]["a%d_%d" % (r, c)])
            piece = T.win[:, _cols(r, c0, c1)]
            rid, pid, _se = topo.addr(d)
            trs.append(RemoteDMATransfer(dst_ids=[DstId(rid=rid, pnc=pid)], dma_engine_mask=_mask(eng),
                                         remote_sem=T.sem["a%d_%d" % (r, c0)], src=piece, dst=piece))
            total += len(eng)
        g.remote_dma_fused(trs, local_sem=T.sem.sent)
    if total:
        g.wait_ge(T.sem.sent, total)


def rank_program(g, core, T, topo):
    cores = list(T.cores)
    rank = T.rank_of(core)
    sends, lands = _plan(cores, topo)
    if rank is None:
        _comms(g, core, T, topo, sends, lands, None)
        return
    sem = T.sem
    nblk = len(BLOCKS)
    lo = [sum(BLOCKS[:i]) for i in range(nblk)]
    ps = [T["ps%d" % i] for i in range(nblk)]

    for c in range(NCH):
        q = g.sync if c % 2 == 0 else g.scalar
        q.dma_start(T.win[:, _cols(rank, c, c + 1)], T.x[:, AT[c]:AT[c + 1]]).then_inc(sem["ldx%d" % c], 16)
    g.sync.dma_start(T.nbi[0:16, :], T.nb[:, :]).then_inc(sem.ldnb, 16)
    g.scalar.dma_start(T.wsb[:, :], T.w[:, :]).then_inc(sem.ldw, 16)

    g.iota(T.iot[0:16, :], [[0, 8], [-4, 8], [-1, 2]], 0, 1, allow_small_or_imprecise_dtypes=True).then_inc(sem.vi, 1)
    _comms(g, core, T, topo, sends, lands, rank)

    v = g.vector
    v.wait_ge(sem.vi, 1)
    for u in range(2):
        for h in range(2):
            i = 2 * u + h
            v.tensor_scalar(T.sel[0:16, i * 128:(i + 1) * 128], T.iot[0:16, :], float(2 * u - 16 * h), None,
                            AluOpType.is_equal).then_inc(sem.vs, 1)
    v.wait_ge(sem.ldnb, 16)
    for h in range(2):
        v.tensor_copy(T.nbf[0:16, h * 128:(h + 1) * 128], T.nbi[0:16, h:256:2]).then_inc(sem.vs, 1)
    pe = g.tensor
    pe.wait_ge(sem.vs, 6)
    for u in range(2):
        for h in range(2):
            i = 2 * u + h
            pe.matmul(T.pso[:, u * 128:(u + 1) * 128], T.sel[0:16, i * 128:(i + 1) * 128],
                      T.nbf[0:16, h * 128:(h + 1) * 128], h == 0, h == 1).then_inc(sem.po, 1)
    v.wait_ge(sem.po, 4)
    v.tensor_copy(T.off[:, :], T.pso[:, 0:256]).then_inc(sem.vo, 1)

    pe.wait_ge(sem.ldw, 16)
    for c in range(NCH):
        pe.wait_ge(sem["ldx%d" % c], 16)
    for i in range(nblk):
        a = rank * V + lo[i]
        pe.matmul(ps[i][:, 0:BLOCKS[i]], T.wsb[:, :], T.win[:, a:a + BLOCKS[i]], True, False).then_inc(sem["pd%d" % i], 1)

    for q in (g.scalar, v):
        q.wait_ge(sem.vo, 1)
        for c in range(NCH):
            q.wait_ge(sem["ldx%d" % c], 16)
        for name in sorted(lands[core]):
            q.wait_ge(sem[name], lands[core][name])
    for i in range(nblk):
        a, b = lo[i], lo[i] + BLOCKS[i]
        first = T.win[:, :].indirect(T.off[:, a // 8:b // 8])
        if i == 0:
            v.tensor_copy(T.gat[:, 2 * a:2 * b], first).then_inc(sem["gd%d" % i], 1)
        else:
            g.scalar.activation(T.gat[:, 2 * a:2 * b], first, ActivationFunctionType.Copy).then_inc(sem["gd%d" % i], 1)
        v.wait_ge(sem["gd%d" % i], 1)
        v.tensor_tensor(T.hsum[:, 2 * a:2 * b], T.win[:, :].indirect(T.off[:, 128 + a // 8:128 + b // 8]),
                        T.gat[:, 2 * a:2 * b], AluOpType.add).then_inc(sem["hd%d" % i], 1)
        pe.wait_ge(sem["hd%d" % i], 1)
        for k in range(2):
            pe.matmul(ps[i][:, 0:BLOCKS[i]], T.wsb[:, :], T.hsum[:, 2 * a + k:2 * b:2], False, k == 1).then_inc(
                sem["pd%d" % i], 1)
    for i in range(nblk):
        a, b = lo[i], lo[i] + BLOCKS[i]
        g.scalar.wait_ge(sem["pd%d" % i], 3)
        g.scalar.activation(T.ysb[:, a:b], ps[i][:, 0:BLOCKS[i]], ActivationFunctionType.Relu).then_inc(sem["rd%d" % i], 1)
    for grp in STORES:
        for i in grp:
            g.sync.wait_ge(sem["rd%d" % i], 1)
        a, b = lo[grp[0]], lo[grp[-1]] + BLOCKS[grp[-1]]
        g.sync.dma_start(T.y[:, a:b], T.ysb[:, a:b]).then_inc(sem.st, 16)
    g.sync.wait_ge(sem.st, 16 * len(STORES))
